import numpy as np
import ml_dtypes


def mxq(x, axis, fmt="e4m3"):
    dtype, down = {"e4m3": (ml_dtypes.float8_e4m3fn, 7), "e5m2": (ml_dtypes.float8_e5m2, 14)}[fmt]
    v = np.moveaxis(np.asarray(x, np.float32).astype(ml_dtypes.bfloat16).astype(np.float64), axis, -1)
    blocks = v.reshape(v.shape[:-1] + (-1, 32))
    amax = np.abs(blocks).max(-1, keepdims=True)
    byte = np.maximum(np.where(amax > 0, np.frexp(amax)[1] - 1 + 127, 0) - down, 1)
    scale = np.exp2(byte - 127.0)
    codes = (blocks / scale).astype(np.float32).astype(dtype).astype(np.float64)
    return np.moveaxis((codes * scale).reshape(v.shape), -1, axis)


WIDE = False


def mx_kscale(k):
    if not WIDE:
        return np.ones(k)
    levels = np.array([10, -10, 5, -5, 0])
    if k % 512:
        return np.exp2(np.random.permutation(np.resize(levels, k // 32))).repeat(32)
    a = np.empty((k // 512, 16))
    for p in range(k // 512):
        a[p, :8] = np.random.permutation(np.resize(levels, 8))
        for g in range(8):
            far = levels[np.abs(levels - a[p, g]) >= 10]
            a[p, g + 8] = far[np.random.randint(len(far))]
    return np.exp2(a.ravel()).repeat(32)


def f64(x):
    return np.asarray(x).astype(np.float64)


def striped(idx):
    return np.tile(np.asarray(idx).reshape(-1, 16).T, (8, 1)).astype(np.uint16)


def unstriped(offs):
    return offs[:16].T.reshape(-1).astype(np.int64)


E2M1 = np.array([0.0, 0.5, 1.0, 1.5, 2.0, 3.0, 4.0, 6.0, -0.0, -0.5, -1.0, -1.5, -2.0, -3.0, -4.0, -6.0])


def pack_weight(w, fmt):
    k, n = w.shape
    w = f64(np.asarray(w, np.float32).astype(ml_dtypes.bfloat16)).reshape(k // 32, 32, n)
    amax = np.abs(w).max(1)
    if fmt == "e4m3":
        byte = np.frexp(amax)[1] - 1 + 127 - 7
    else:
        mant, ex = np.frexp(amax / 6.0)
        byte = np.where(mant > 0.5, ex, ex - 1) + 127
    byte = np.clip(np.where(amax > 0, byte, 1), 1, 254)
    scaled = (w * np.exp2(127.0 - byte)[:, None, :]).reshape(k, n).astype(np.float32)
    by_word = np.ascontiguousarray(scaled.reshape(k // 512, 128, 4, n).transpose(0, 1, 3, 2))
    if fmt == "e4m3":
        words = by_word.astype(ml_dtypes.float8_e4m3fn).view(np.uint8)
    else:
        c = by_word.astype(ml_dtypes.float4_e2m1fn).view(np.uint8) & 0xF
        words = (c[..., 0::2] | (c[..., 1::2] << 4)).reshape(k // 512, 128, 2 * n)
    return np.ascontiguousarray(words), np.ascontiguousarray(byte.astype(np.uint8).reshape(k // 512, 16, n))


def unpack_weight(words, scales, fmt):
    g, _, n = scales.shape
    words = np.ascontiguousarray(words).reshape(g, 128, n, -1)
    if fmt == "e4m3":
        vals = words.view(ml_dtypes.float8_e4m3fn).astype(np.float64)
    else:
        nib = np.empty((g, 128, n, 4), np.uint8)
        nib[..., 0::2] = words & 0xF
        nib[..., 1::2] = words >> 4
        vals = E2M1[nib]
    vals = vals * np.repeat(np.exp2(scales.astype(np.float64) - 127.0), 8, axis=1)[..., None]
    return vals.transpose(0, 1, 3, 2).reshape(g * 512, n)


def sigmoid(v):
    return 1.0 / (1.0 + np.exp(-v))


D, E, T, I, Q = 512, 512, 2048, 512, 128


def setup_inputs():
    n = np.random.standard_normal
    idx = np.random.permutation(T)[:I]
    fd = mx_kscale(D)
    fe = mx_kscale(E)
    keysp = pack_weight(n((D, T)) / fd[:, None], "e4m3")
    valsp = pack_weight(n((E, T)) / fe[:, None], "e4m3")
    return {
        "query": (n((D, Q)) * 0.5 / np.sqrt(D) * fd[:, None]).astype(np.float32),
        "query2": (n((D, Q)) * 0.6 / np.sqrt(D) * fd[:, None]).astype(np.float32),
        "keys_words": keysp[0],
        "keys_scales": keysp[1],
        "age": np.tile(np.random.uniform(0.0, 2.0, T), (128, 1)).astype(np.float32),
        "grace": (np.random.uniform(0.7, 1.5, (Q, 1))).astype(np.float32),
        "gout": (n((E, Q)) * 1 / np.sqrt(E) * fe[:, None]).astype(np.float32),
        "vals_words": valsp[0],
        "vals_scales": valsp[1],
        "size": (np.random.uniform(0.5, 2.0, (1, I))).astype(np.float32),
        "base": (0.5 * n((Q, T))).astype(np.float32),
        "gq1": (np.random.uniform(0.3, 1.5, (Q, 1))).astype(np.float32),
        "offs": striped(idx),
    }


def reference(query, query2, keys_words, keys_scales, age, grace, gout, vals_words, vals_scales, size, base, gq1, offs):
    idx = unstriped(offs)
    keysu = unpack_weight(keys_words, keys_scales, "e4m3")
    valsu = unpack_weight(vals_words, vals_scales, "e4m3")
    queryq = mxq(f64(query), 0, "e4m3")
    keysidxg = keysu[:, idx]
    a = queryq.T @ keysidxg
    query2q = mxq(f64(query2), 0, "e4m3")
    b = query2q.T @ keysidxg
    r = np.exp(a - np.max(a, axis=1, keepdims=True))
    gt = sigmoid((b + f64(grace) - f64(age)[:1][:, idx]) * 3.0)
    p = r * gt
    z = np.sum(p, axis=1, keepdims=True)
    goutq = mxq(f64(gout), 0, "e4m3")
    valsidxg = valsu[:, idx]
    c0 = goutq.T @ valsidxg
    dz = np.sum(c0 * p * f64(size) / np.square(z) * (-1.0), axis=1, keepdims=True)
    dp = c0 / z * f64(size) + dz
    dgt = dp * r
    db = dgt * gt * (1.0 - gt) * 3.0
    hdb = db * 512.0 * 2.0 * 512.0
    hdgt = hdb * 3.0 * (1.0 - gt) * gt
    hdp = hdgt * r
    hdz = np.sum(hdp, axis=1, keepdims=True)
    hz = np.sum(hdp * f64(size) * c0 / np.square(z) * (-1.0), axis=1, keepdims=True) + np.sum(hdz * (-1.0) * c0 * p * f64(size) / np.square(np.square(z)) * (-1.0), axis=1, keepdims=True) * z * 2.0
    hp = hdz * (-1.0) / np.square(z) * c0 * f64(size) + hz
    hgt = hdb * 3.0 * (1.0 - gt) * dgt + hp * r - hdb * 3.0 * dgt * gt
    hb = hgt * gt * (1.0 - gt) * 3.0
    gs = hb * f64(gq1)
    gf = np.zeros((Q, T))
    gf[:, idx] = gs
    y = f64(base) + gf
    return y

@@ -1,0 +1,204 @@
+from contextlib import ExitStack
+
+import concourse.mybir as mybir
+from concourse.masks import make_identity
+
+D, E, T, I, Q = 512, 512, 2048, 512, 128
+FLOPS = 3 * 2 * 512 * 512 * 128
+
+F32 = mybir.dt.float32
+BF16 = mybir.dt.bfloat16
+I32 = mybir.dt.int32
+U32 = mybir.dt.uint32
+U16 = mybir.dt.uint16
+U8 = mybir.dt.uint8
+FP8X4 = mybir.dt.float8_e4m3fn_x4
+ALU = mybir.AluOpType
+ACT = mybir.ActivationFunctionType
+AX = mybir.AxisListType
+
+P = 128
+PACK = 4
+PENALTY = 27.0 * 2.0 * 512.0 * 512.0
+STORE_WIDTHS = [256, 512, 512, 512, 256]
+
+
+def tile_attend_gpsoftlives_b_kernel(tc, query, query2, keys_words, keys_scales, age, grace, gout,
+                                      vals_words, vals_scales, size, base, gq1, offs, out):
+    nc = tc.nc
+    with ExitStack() as ctx:
+        sb = ctx.enter_context(tc.tile_pool(name="sb", bufs=1))
+        ps = ctx.enter_context(tc.psum_pool(name="ps", bufs=1))
+
+        offsets = sb.tile([P, I // 16], U16, name="offsets")
+        nc.sync.dma_start(offsets[:], offs)
+
+        ident = sb.tile([P, P], F32, name="ident")
+        make_identity(nc, ident[:])
+
+        key_bytes = sb.tile([P, T], U8, name="key_bytes", align_bytes=64)
+        val_bytes = sb.tile([P, T], U8, name="val_bytes", align_bytes=64)
+        age_pool = sb.tile([P, T], F32, name="age_pool")
+        zeros = sb.tile([P, 1], F32, name="zeros", tag="late_a", align_bytes=64)
+        placed = sb.tile([P, T], F32, name="placed")
+        nc.vector.memset(key_bytes[:].bitcast(I32), 0)
+        nc.vector.memset(val_bytes[:].bitcast(I32), 0)
+        nc.vector.memset(age_pool[:], 0.0)
+        nc.vector.memset(zeros[:], 0.0)
+        nc.vector.memset(placed[:], 0.0)
+
+        key_words = sb.tile([P, T], I32, name="key_words", align_bytes=64)
+        nc.sync.dma_start(key_words[:], keys_words[0].rearrange("p n t -> p (n t)").bitcast(I32))
+        query_raw = sb.tile([P, PACK, Q], F32, name="query_raw", tag="raw_a")
+        nc.sync.dma_start(query_raw[:], query.rearrange("(p j) w -> p j w", j=PACK))
+        query2_raw = sb.tile([P, PACK, Q], F32, name="query2_raw")
+        nc.sync.dma_start(query2_raw[:], query2.rearrange("(p j) w -> p j w", j=PACK))
+
+        def load_scale_rows(queue, tile, scales):
+            for quad in range(4):
+                queue.dma_start(tile[32 * quad : 32 * quad + 4, :].bitcast(I32),
+                                scales[0, 4 * quad : 4 * quad + 4, :].bitcast(I32))
+
+        load_scale_rows(nc.scalar, key_bytes, keys_scales)
+        nc.scalar.dma_start(age_pool[0:1, :], age[0:1, :])
+
+        size_cols = sb.tile([P, PACK], F32, name="size_cols")
+        nc.gpsimd.dma_start(size_cols[:], size.rearrange("o (p j) -> (o p) j", j=PACK))
+        grace_col = sb.tile([P, 1], F32, name="grace_col")
+        nc.gpsimd.dma_start(grace_col[:], grace)
+        load_scale_rows(nc.gpsimd, val_bytes, vals_scales)
+        gq1_col = sb.tile([P, 1], F32, name="gq1_col")
+        nc.gpsimd.dma_start(gq1_col[:], gq1)
+
+        warm = sb.tile([P, 1], F32, name="warm")
+        nc.scalar.activation(warm[:], zeros[:, 0:1], ACT.Exp)
+
+        val_words = sb.tile([P, T], I32, name="val_words", tag="late_a", align_bytes=64)
+        nc.sync.dma_start(val_words[:], vals_words[0].rearrange("p n t -> p (n t)").bitcast(I32))
+
+        def quantize(raw, name):
+            grouped = sb.tile([P, Q, PACK], BF16, name=name + "_grouped", align_bytes=64)
+            nc.scalar.copy(grouped[:].rearrange("p (c i) t -> p c t i", i=4),
+                           raw[:].rearrange("p t (c i) -> p c t i", i=4))
+            codes = sb.tile([P, Q], U32, name=name + "_codes", align_bytes=64)
+            scales = sb.tile([P, Q], U8, name=name + "_scales", align_bytes=64)
+            nc.vector.quantize_mx(out=codes[:].bitcast(FP8X4), scales=scales[:],
+                                  in_=grouped[:].rearrange("p w j -> p (w j)"))
+            return codes, scales
+
+        def gather(window, dtype, name):
+            picked = sb.tile([P, I], dtype, name=name, align_bytes=64)
+            nc.vector.tensor_copy(picked[:], window.indirect(offsets[:]))
+            return picked
+
+        def scores(rows, words, scale_bytes, name):
+            bank = ps.tile([P, I], F32, name=name)
+            nc.tensor.matmul_mx(out=bank[:], lhsT=rows[0][:].bitcast(FP8X4), lhsT_scale=rows[1][:],
+                                rhs=words[:].bitcast(FP8X4), rhs_scale=scale_bytes[:], start=True, stop=True)
+            return bank
+
+        def column(name):
+            return sb.tile([P, 1], F32, name=name)
+
+        def row_tile(name):
+            return sb.tile([P, I], F32, name=name)
+
+        size_bank = ps.tile([P, PACK, P], F32, name="size_bank")
+        for j in range(PACK):
+            nc.tensor.transpose(size_bank[:, j, :], size_cols[:, j : j + 1].to_broadcast([P, P]), ident[:])
+        size_rows = sb.tile([P, P, PACK], F32, name="size_rows")
+        nc.scalar.copy(size_rows[:], size_bank[:].rearrange("p j s -> p s j"))
+
+        key_bytes_g = gather(key_bytes[:], U8, "key_bytes_g")
+        key_words_g = gather(key_words[:].bitcast(U32), U32, "key_words_g")
+        query_mx = quantize(query_raw, "query")
+        a_bank = scores(query_mx, key_words_g, key_bytes_g, "a_bank")
+        query2_mx = quantize(query2_raw, "query2")
+        b_bank = scores(query2_mx, key_words_g, key_bytes_g, "b_bank")
+
+        gout_raw = sb.tile([P, PACK, Q], F32, name="gout_raw", tag="raw_a")
+        nc.sync.dma_start(gout_raw[:], gout.rearrange("(p j) w -> p j w", j=PACK))
+
+        age_g = gather(age_pool[:], F32, "age_g")
+        age_turn = ps.tile([P, PACK, P], F32, name="age_turn")
+        for j in range(PACK):
+            nc.tensor.transpose(age_turn[:, j, :], age_g[:, j * P : (j + 1) * P], ident[:])
+        age_cols = sb.tile([P, PACK], F32, name="age_cols")
+        nc.scalar.copy(age_cols[:], age_turn[:, :, 0])
+        age_bank = ps.tile([P, PACK, P], F32, name="age_bank")
+        for j in range(PACK):
+            nc.tensor.transpose(age_bank[:, j, :], age_cols[:, j : j + 1].to_broadcast([P, P]), ident[:])
+        slack = row_tile("slack")
+        nc.scalar.activation(slack[:], age_bank[:].rearrange("p j s -> p (j s)"), ACT.Identity,
+                             bias=grace_col[:], scale=-1.0)
+
+        neg_max = column("neg_max")
+        nc.vector.tensor_reduce(neg_max[:], a_bank[:], AX.X, ALU.max, negate=True)
+        r = row_tile("r")
+        nc.scalar.activation(r[:], a_bank[:], ACT.Exp, bias=neg_max[:])
+
+        x = row_tile("x")
+        nc.vector.tensor_tensor(x[:], b_bank[:], slack[:], ALU.add)
+        life = row_tile("life")
+        nc.scalar.activation(life[:], x[:], ACT.Sigmoid, scale=3.0)
+        death = row_tile("death")
+        nc.scalar.activation(death[:], x[:], ACT.Sigmoid, scale=-3.0)
+
+        val_bytes_g = gather(val_bytes[:], U8, "val_bytes_g")
+        val_words_g = gather(val_words[:].bitcast(U32), U32, "val_words_g")
+        gout_mx = quantize(gout_raw, "gout")
+        c_bank = scores(gout_mx, val_words_g, val_bytes_g, "c_bank")
+
+        base_sb = sb.tile([P, T], F32, name="base_sb", tag="late_a", align_bytes=64)
+        nc.sync.dma_start(base_sb[:], base)
+
+        gain = column("gain")
+        nc.gpsimd.tensor_scalar(gain[:], gq1_col[:], PENALTY, 0.0, ALU.mult, ALU.add)
+        neg_gain = column("neg_gain")
+        nc.gpsimd.tensor_scalar(neg_gain[:], gq1_col[:], -PENALTY, 0.0, ALU.mult, ALU.add)
+        neg_two_gain = column("neg_two_gain")
+        nc.gpsimd.tensor_scalar(neg_two_gain[:], gq1_col[:], -2.0 * PENALTY, 0.0, ALU.mult, ALU.add)
+
+        c = row_tile("c")
+        nc.vector.tensor_tensor(c[:], c_bank[:], size_rows[:].rearrange("p s j -> p (s j)"), ALU.mult)
+
+        p = row_tile("p")
+        z = column("z")
+        nc.vector.scalar_tensor_tensor(p[:], r[:], 1.0, life[:], ALU.mult, ALU.mult, accum_out=z[:])
+        inv_z = column("inv_z")
+        nc.vector.reciprocal(inv_z[:], z[:])
+        bend = row_tile("bend")
+        nc.scalar.activation(bend[:], life[:], ACT.Identity, bias=gain[:], scale=neg_two_gain[:])
+
+        mean = column("mean")
+        cp = row_tile("cp")
+        nc.vector.scalar_tensor_tensor(cp[:], p[:], inv_z[:], c[:], ALU.mult, ALU.mult, accum_out=mean[:])
+        u = row_tile("u")
+        nc.vector.scalar_tensor_tensor(u[:], p[:], inv_z[:], death[:], ALU.mult, ALU.mult)
+        v = row_tile("v")
+        nc.vector.scalar_tensor_tensor(v[:], c[:], mean[:], u[:], ALU.subtract, ALU.mult)
+        gain_u = row_tile("gain_u")
+        nc.scalar.activation(gain_u[:], u[:], ACT.Copy, scale=neg_gain[:])
+
+        sum_vv = column("sum_vv")
+        vv = row_tile("vv")
+        nc.scalar.activation(vv[:], v[:], ACT.Square, accum_out=sum_vv[:])
+        tail = row_tile("tail")
+        nc.scalar.activation(tail[:], gain_u[:], ACT.Copy, scale=sum_vv[:])
+
+        sum_vu = column("sum_vu")
+        vu = row_tile("vu")
+        nc.vector.scalar_tensor_tensor(vu[:], v[:], neg_gain[:], u[:], ALU.mult, ALU.mult, accum_out=sum_vu[:])
+        k = row_tile("k")
+        nc.vector.tensor_tensor(k[:], v[:], bend[:], ALU.mult)
+        head = row_tile("head")
+        nc.vector.scalar_tensor_tensor(head[:], k[:], sum_vu[:], v[:], ALU.add, ALU.mult)
+        nc.vector.tensor_tensor(placed[:].indirect(offsets[:]), head[:], tail[:], ALU.add)
+
+        start = 0
+        for n, width in enumerate(STORE_WIDTHS):
+            cols = slice(start, start + width)
+            total = sb.tile([P, width], F32, name="total%d" % n)
+            nc.vector.tensor_tensor(total[:], placed[:, cols], base_sb[:, cols], ALU.add)
+            nc.sync.dma_start(out[:, cols], total[:])
+            start = start + width

@@ -1,7 +1,6 @@
 from contextlib import ExitStack
 
 import concourse.mybir as mybir
-from concourse.masks import make_identity
 
 D, E, T, I, Q = 512, 512, 2048, 512, 128
 FLOPS = 3 * 2 * 512 * 512 * 128
@@ -33,148 +32,150 @@ def tile_attend_gpsoftlives_b_kernel(tc, query, query2, keys_words, keys_scales,
         offsets = sb.tile([P, I // 16], U16, name="offsets")
         nc.sync.dma_start(offsets[:], offs)
 
-        ident = sb.tile([P, P], F32, name="ident")
-        make_identity(nc, ident[:])
+        size_cols = sb.tile([P, PACK], F32, name="size_cols")
+        nc.sync.dma_start(size_cols[:], size.rearrange("o (p j) -> (o p) j", j=PACK))
+        query_raw = sb.tile([P, PACK, Q], F32, name="query_raw")
+        nc.sync.dma_start(query_raw[:], query.rearrange("(p j) w -> p j w", j=PACK))
 
         key_bytes = sb.tile([P, T], U8, name="key_bytes", align_bytes=64)
-        val_bytes = sb.tile([P, T], U8, name="val_bytes", align_bytes=64)
-        age_pool = sb.tile([P, T], F32, name="age_pool")
-        zeros = sb.tile([P, 1], F32, name="zeros", tag="late_a", align_bytes=64)
-        placed = sb.tile([P, T], F32, name="placed")
-        nc.vector.memset(key_bytes[:].bitcast(I32), 0)
-        nc.vector.memset(val_bytes[:].bitcast(I32), 0)
-        nc.vector.memset(age_pool[:], 0.0)
-        nc.vector.memset(zeros[:], 0.0)
-        nc.vector.memset(placed[:], 0.0)
+        val_bytes = sb.tile([P, T], U8, name="val_bytes", tag="val_bytes", align_bytes=64)
+        age_pool = sb.tile([P, T], F32, name="age_pool", tag="age_pool", align_bytes=64)
+        nc.gpsimd.memset(key_bytes[:].bitcast(I32), 0)
+        nc.gpsimd.memset(age_pool[:], 0.0)
+        nc.gpsimd.memset(val_bytes[:].bitcast(I32), 0)
 
-        key_words = sb.tile([P, T], I32, name="key_words", align_bytes=64)
+        def load_scale_rows(tile, scales):
+            for quad in range(4):
+                nc.sync.dma_start(tile[32 * quad : 32 * quad + 4, :].bitcast(I32),
+                                  scales[0, 4 * quad : 4 * quad + 4, :].bitcast(I32))
+
+        load_scale_rows(key_bytes, keys_scales)
+        key_words = sb.tile([P, T], I32, name="key_words", tag="key_words", align_bytes=64)
         nc.sync.dma_start(key_words[:], keys_words[0].rearrange("p n t -> p (n t)").bitcast(I32))
-        query_raw = sb.tile([P, PACK, Q], F32, name="query_raw", tag="raw_a")
-        nc.sync.dma_start(query_raw[:], query.rearrange("(p j) w -> p j w", j=PACK))
+        nc.sync.dma_start(age_pool[0:1, :], age[0:1, :])
         query2_raw = sb.tile([P, PACK, Q], F32, name="query2_raw")
         nc.sync.dma_start(query2_raw[:], query2.rearrange("(p j) w -> p j w", j=PACK))
-
-        def load_scale_rows(queue, tile, scales):
-            for quad in range(4):
-                queue.dma_start(tile[32 * quad : 32 * quad + 4, :].bitcast(I32),
-                                scales[0, 4 * quad : 4 * quad + 4, :].bitcast(I32))
-
-        load_scale_rows(nc.scalar, key_bytes, keys_scales)
-        nc.scalar.dma_start(age_pool[0:1, :], age[0:1, :])
-
-        size_cols = sb.tile([P, PACK], F32, name="size_cols")
-        nc.gpsimd.dma_start(size_cols[:], size.rearrange("o (p j) -> (o p) j", j=PACK))
-        grace_col = sb.tile([P, 1], F32, name="grace_col")
-        nc.gpsimd.dma_start(grace_col[:], grace)
-        load_scale_rows(nc.gpsimd, val_bytes, vals_scales)
-        gq1_col = sb.tile([P, 1], F32, name="gq1_col")
-        nc.gpsimd.dma_start(gq1_col[:], gq1)
-
-        warm = sb.tile([P, 1], F32, name="warm")
-        nc.scalar.activation(warm[:], zeros[:, 0:1], ACT.Exp)
-
-        val_words = sb.tile([P, T], I32, name="val_words", tag="late_a", align_bytes=64)
+        gout_raw = sb.tile([P, PACK, Q], F32, name="gout_raw", tag="gout_raw", align_bytes=64)
+        nc.sync.dma_start(gout_raw[:], gout.rearrange("(p j) w -> p j w", j=PACK))
+        load_scale_rows(val_bytes, vals_scales)
+        val_words = sb.tile([P, T], I32, name="val_words", tag="val_words", align_bytes=64)
         nc.sync.dma_start(val_words[:], vals_words[0].rearrange("p n t -> p (n t)").bitcast(I32))
+        grace_col = sb.tile([P, 1], F32, name="grace_col")
+        nc.sync.dma_start(grace_col[:], grace)
+        gq1_col = sb.tile([P, 1], F32, name="gq1_col")
+        nc.sync.dma_start(gq1_col[:], gq1)
+        base_sb = sb.tile([P, T], F32, name="base_sb")
+        nc.sync.dma_start(base_sb[:], base)
 
-        def quantize(raw, name):
-            grouped = sb.tile([P, Q, PACK], BF16, name=name + "_grouped", align_bytes=64)
+        ones = sb.tile([P, P], F32, name="ones")
+        nc.vector.memset(ones[:], 1.0)
+        warm = sb.tile([P, 1], F32, name="warm")
+        nc.scalar.activation(warm[:], ones[:, 0:1], ACT.Exp)
+        quad_start = sb.tile([P, 1], F32, name="quad_start")
+        for quad in range(4):
+            nc.vector.memset(quad_start[32 * quad : 32 * quad + 32, :], 32.0 * quad)
+        count = sb.tile([P, P], F32, name="count", align_bytes=64)
+        nc.vector.tensor_tensor_scan(count[:], ones[:], ones[:], 0.0, ALU.mult, ALU.add)
+        lane = sb.tile([P, 32], F32, name="lane", align_bytes=64)
+        nc.vector.transpose(lane[:], count[:, 0:32])
+        ident = sb.tile([P, P], F32, name="ident")
+        nc.vector.scalar_tensor_tensor(ident[:], count[:], quad_start[:], lane[:, 0:1].to_broadcast([P, P]),
+                                       ALU.subtract, ALU.is_equal)
+
+        def quantize(raw, name, tag, codes_tag):
+            grouped = sb.tile([P, Q, PACK], BF16, name=name + "_grouped", tag=tag, align_bytes=64)
             nc.scalar.copy(grouped[:].rearrange("p (c i) t -> p c t i", i=4),
                            raw[:].rearrange("p t (c i) -> p c t i", i=4))
-            codes = sb.tile([P, Q], U32, name=name + "_codes", align_bytes=64)
-            scales = sb.tile([P, Q], U8, name=name + "_scales", align_bytes=64)
+            codes = sb.tile([P, Q], U32, name=name + "_codes", tag=codes_tag, align_bytes=64)
+            scales = sb.tile([P, Q], U8, name=name + "_scales", tag=name + "_scales", align_bytes=64)
             nc.vector.quantize_mx(out=codes[:].bitcast(FP8X4), scales=scales[:],
                                   in_=grouped[:].rearrange("p w j -> p (w j)"))
             return codes, scales
 
-        def gather(window, dtype, name):
-            picked = sb.tile([P, I], dtype, name=name, align_bytes=64)
+        def gather(window, dtype, name, tag=None):
+            picked = sb.tile([P, I], dtype, name=name, tag=tag or name, align_bytes=64)
             nc.vector.tensor_copy(picked[:], window.indirect(offsets[:]))
             return picked
 
         def scores(rows, words, scale_bytes, name):
-            bank = ps.tile([P, I], F32, name=name)
+            bank = ps.tile([P, I], F32, name=name, tag=name)
             nc.tensor.matmul_mx(out=bank[:], lhsT=rows[0][:].bitcast(FP8X4), lhsT_scale=rows[1][:],
                                 rhs=words[:].bitcast(FP8X4), rhs_scale=scale_bytes[:], start=True, stop=True)
             return bank
 
-        def column(name):
-            return sb.tile([P, 1], F32, name=name)
+        def column(name, tag=None):
+            return sb.tile([P, 1], F32, name=name, tag=tag or name, align_bytes=64)
 
-        def row_tile(name):
-            return sb.tile([P, I], F32, name=name)
+        def row_tile(name, tag=None):
+            return sb.tile([P, I], F32, name=name, tag=tag or name, align_bytes=64)
 
-        size_bank = ps.tile([P, PACK, P], F32, name="size_bank")
+        key_bytes_g = gather(key_bytes[:], U8, "key_bytes_g")
+        query_mx = quantize(query_raw, "query", "key_words_g", "query_codes")
+
+        size_bank = ps.tile([P, PACK, P], F32, name="size_bank", tag="a_bank")
         for j in range(PACK):
             nc.tensor.transpose(size_bank[:, j, :], size_cols[:, j : j + 1].to_broadcast([P, P]), ident[:])
         size_rows = sb.tile([P, P, PACK], F32, name="size_rows")
         nc.scalar.copy(size_rows[:], size_bank[:].rearrange("p j s -> p s j"))
 
-        key_bytes_g = gather(key_bytes[:], U8, "key_bytes_g")
         key_words_g = gather(key_words[:].bitcast(U32), U32, "key_words_g")
-        query_mx = quantize(query_raw, "query")
         a_bank = scores(query_mx, key_words_g, key_bytes_g, "a_bank")
-        query2_mx = quantize(query2_raw, "query2")
+        age_g = gather(age_pool[:], F32, "age_g", "key_words")
+        query2_mx = quantize(query2_raw, "query2", "query2_grouped", "age_pool")
         b_bank = scores(query2_mx, key_words_g, key_bytes_g, "b_bank")
 
-        gout_raw = sb.tile([P, PACK, Q], F32, name="gout_raw", tag="raw_a")
-        nc.sync.dma_start(gout_raw[:], gout.rearrange("(p j) w -> p j w", j=PACK))
-
-        age_g = gather(age_pool[:], F32, "age_g")
         age_turn = ps.tile([P, PACK, P], F32, name="age_turn")
         for j in range(PACK):
             nc.tensor.transpose(age_turn[:, j, :], age_g[:, j * P : (j + 1) * P], ident[:])
-        age_cols = sb.tile([P, PACK], F32, name="age_cols")
+        age_cols = sb.tile([P, PACK], F32, name="age_cols", tag="query2_scales", align_bytes=64)
         nc.scalar.copy(age_cols[:], age_turn[:, :, 0])
         age_bank = ps.tile([P, PACK, P], F32, name="age_bank")
         for j in range(PACK):
             nc.tensor.transpose(age_bank[:, j, :], age_cols[:, j : j + 1].to_broadcast([P, P]), ident[:])
-        slack = row_tile("slack")
-        nc.scalar.activation(slack[:], age_bank[:].rearrange("p j s -> p (j s)"), ACT.Identity,
-                             bias=grace_col[:], scale=-1.0)
 
-        neg_max = column("neg_max")
-        nc.vector.tensor_reduce(neg_max[:], a_bank[:], AX.X, ALU.max, negate=True)
-        r = row_tile("r")
+        neg_max = column("neg_max", "query2_grouped")
+        neg_a = row_tile("neg_a")
+        nc.vector.tensor_scalar(neg_a[:], a_bank[:], -1.0, None, ALU.mult, ALU.min, accum_out=neg_max[:])
+        r = row_tile("r", "gout_raw")
+        b = row_tile("b")
+        val_bytes_g = gather(val_bytes[:], U8, "val_bytes_g", "neg_a")
+        gout_mx = quantize(gout_raw, "gout", "gout_grouped", "val_bytes")
         nc.scalar.activation(r[:], a_bank[:], ACT.Exp, bias=neg_max[:])
+        nc.scalar.copy(b[:], b_bank[:])
 
-        x = row_tile("x")
-        nc.vector.tensor_tensor(x[:], b_bank[:], slack[:], ALU.add)
+        x = row_tile("x", "gout_grouped")
+        nc.vector.scalar_tensor_tensor(x[:], b[:], grace_col[:], age_bank[:].rearrange("p j s -> p (j s)"),
+                                       ALU.add, ALU.subtract)
         life = row_tile("life")
         nc.scalar.activation(life[:], x[:], ACT.Sigmoid, scale=3.0)
         death = row_tile("death")
         nc.scalar.activation(death[:], x[:], ACT.Sigmoid, scale=-3.0)
 
-        val_bytes_g = gather(val_bytes[:], U8, "val_bytes_g")
-        val_words_g = gather(val_words[:].bitcast(U32), U32, "val_words_g")
-        gout_mx = quantize(gout_raw, "gout")
+        val_words_g = gather(val_words[:].bitcast(U32), U32, "val_words_g", "b")
         c_bank = scores(gout_mx, val_words_g, val_bytes_g, "c_bank")
 
-        base_sb = sb.tile([P, T], F32, name="base_sb", tag="late_a", align_bytes=64)
-        nc.sync.dma_start(base_sb[:], base)
+        placed = sb.tile([P, T], F32, name="placed", tag="b", align_bytes=64)
+        nc.gpsimd.memset(placed[:], 0.0)
 
-        gain = column("gain")
-        nc.gpsimd.tensor_scalar(gain[:], gq1_col[:], PENALTY, 0.0, ALU.mult, ALU.add)
         neg_gain = column("neg_gain")
-        nc.gpsimd.tensor_scalar(neg_gain[:], gq1_col[:], -PENALTY, 0.0, ALU.mult, ALU.add)
-        neg_two_gain = column("neg_two_gain")
-        nc.gpsimd.tensor_scalar(neg_two_gain[:], gq1_col[:], -2.0 * PENALTY, 0.0, ALU.mult, ALU.add)
+        nc.scalar.activation(neg_gain[:], gq1_col[:], ACT.Copy, scale=-PENALTY)
 
-        c = row_tile("c")
-        nc.vector.tensor_tensor(c[:], c_bank[:], size_rows[:].rearrange("p s j -> p (s j)"), ALU.mult)
-
-        p = row_tile("p")
+        p = row_tile("p", "val_words")
         z = column("z")
         nc.vector.scalar_tensor_tensor(p[:], r[:], 1.0, life[:], ALU.mult, ALU.mult, accum_out=z[:])
         inv_z = column("inv_z")
         nc.vector.reciprocal(inv_z[:], z[:])
         bend = row_tile("bend")
-        nc.scalar.activation(bend[:], life[:], ACT.Identity, bias=gain[:], scale=neg_two_gain[:])
+        nc.scalar.activation(bend[:], life[:], ACT.Identity, bias=-1.0, scale=2.0)
 
+        c = row_tile("c", "gout_raw")
+        nc.vector.tensor_tensor(c[:], c_bank[:], size_rows[:].rearrange("p s j -> p (s j)"), ALU.mult)
+
+        u = row_tile("u")
+        nc.vector.scalar_tensor_tensor(u[:], p[:], inv_z[:], death[:], ALU.mult, ALU.mult)
         mean = column("mean")
         cp = row_tile("cp")
         nc.vector.scalar_tensor_tensor(cp[:], p[:], inv_z[:], c[:], ALU.mult, ALU.mult, accum_out=mean[:])
-        u = row_tile("u")
-        nc.vector.scalar_tensor_tensor(u[:], p[:], inv_z[:], death[:], ALU.mult, ALU.mult)
         v = row_tile("v")
         nc.vector.scalar_tensor_tensor(v[:], c[:], mean[:], u[:], ALU.subtract, ALU.mult)
         gain_u = row_tile("gain_u")
@@ -190,7 +191,7 @@ def tile_attend_gpsoftlives_b_kernel(tc, query, query2, keys_words, keys_scales,
         vu = row_tile("vu")
         nc.vector.scalar_tensor_tensor(vu[:], v[:], neg_gain[:], u[:], ALU.mult, ALU.mult, accum_out=sum_vu[:])
         k = row_tile("k")
-        nc.vector.tensor_tensor(k[:], v[:], bend[:], ALU.mult)
+        nc.vector.scalar_tensor_tensor(k[:], v[:], neg_gain[:], bend[:], ALU.mult, ALU.mult)
         head = row_tile("head")
         nc.vector.scalar_tensor_tensor(head[:], k[:], sum_vu[:], v[:], ALU.add, ALU.mult)
         nc.vector.tensor_tensor(placed[:].indirect(offsets[:]), head[:], tail[:], ALU.add)

@@ -14,11 +14,11 @@ U8 = mybir.dt.uint8
 FP8X4 = mybir.dt.float8_e4m3fn_x4
 ALU = mybir.AluOpType
 ACT = mybir.ActivationFunctionType
-AX = mybir.AxisListType
 
 P = 128
 PACK = 4
 PENALTY = 27.0 * 2.0 * 512.0 * 512.0
+AGE_SPLIT = 1024
 STORE_WIDTHS = [256, 512, 512, 512, 256]
 
 
@@ -27,6 +27,7 @@ def tile_attend_gpsoftlives_b_kernel(tc, query, query2, keys_words, keys_scales,
     nc = tc.nc
     with ExitStack() as ctx:
         sb = ctx.enter_context(tc.tile_pool(name="sb", bufs=1))
+        reuse = ctx.enter_context(tc.tile_pool(name="reuse", bufs=1))
         ps = ctx.enter_context(tc.psum_pool(name="ps", bufs=1))
 
         offsets = sb.tile([P, I // 16], U16, name="offsets")
@@ -34,14 +35,19 @@ def tile_attend_gpsoftlives_b_kernel(tc, query, query2, keys_words, keys_scales,
 
         size_cols = sb.tile([P, PACK], F32, name="size_cols")
         nc.sync.dma_start(size_cols[:], size.rearrange("o (p j) -> (o p) j", j=PACK))
-        query_raw = sb.tile([P, PACK, Q], F32, name="query_raw")
-        nc.sync.dma_start(query_raw[:], query.rearrange("(p j) w -> p j w", j=PACK))
+
+        ones = sb.tile([P, P], F32, name="ones")
+        nc.vector.memset(ones[:], 1.0)
+        warm = sb.tile([P, 1], F32, name="warm")
+        nc.scalar.activation(warm[:], ones[:, 0:1], ACT.Exp)
 
         key_bytes = sb.tile([P, T], U8, name="key_bytes", align_bytes=64)
         val_bytes = sb.tile([P, T], U8, name="val_bytes", tag="val_bytes", align_bytes=64)
-        age_pool = sb.tile([P, T], F32, name="age_pool", tag="age_pool", align_bytes=64)
+        age_pool = reuse.tile([P, T], F32, name="age_pool", align_bytes=64, offset=0)
         nc.gpsimd.memset(key_bytes[:].bitcast(I32), 0)
-        nc.gpsimd.memset(age_pool[:], 0.0)
+        nc.vector.memset(age_pool[:, : AGE_SPLIT - 1], 0.0)
+        nc.vector.memset(age_pool[:, AGE_SPLIT - 1 : AGE_SPLIT], 0.0)
+        nc.gpsimd.memset(age_pool[:, AGE_SPLIT:], 0.0)
         nc.gpsimd.memset(val_bytes[:].bitcast(I32), 0)
 
         def load_scale_rows(tile, scales):
@@ -50,27 +56,25 @@ def tile_attend_gpsoftlives_b_kernel(tc, query, query2, keys_words, keys_scales,
                                   scales[0, 4 * quad : 4 * quad + 4, :].bitcast(I32))
 
         load_scale_rows(key_bytes, keys_scales)
-        key_words = sb.tile([P, T], I32, name="key_words", tag="key_words", align_bytes=64)
-        nc.sync.dma_start(key_words[:], keys_words[0].rearrange("p n t -> p (n t)").bitcast(I32))
+        query_raw = sb.tile([P, PACK, Q], F32, name="query_raw")
+        nc.sync.dma_start(query_raw[:], query.rearrange("(p j) w -> p j w", j=PACK))
         nc.sync.dma_start(age_pool[0:1, :], age[0:1, :])
-        query2_raw = sb.tile([P, PACK, Q], F32, name="query2_raw")
-        nc.sync.dma_start(query2_raw[:], query2.rearrange("(p j) w -> p j w", j=PACK))
-        gout_raw = sb.tile([P, PACK, Q], F32, name="gout_raw", tag="gout_raw", align_bytes=64)
-        nc.sync.dma_start(gout_raw[:], gout.rearrange("(p j) w -> p j w", j=PACK))
+        key_words = sb.tile([P, T], I32, name="key_words", align_bytes=64)
+        nc.sync.dma_start(key_words[:], keys_words[0].rearrange("p n t -> p (n t)").bitcast(I32))
         load_scale_rows(val_bytes, vals_scales)
-        val_words = sb.tile([P, T], I32, name="val_words", tag="val_words", align_bytes=64)
-        nc.sync.dma_start(val_words[:], vals_words[0].rearrange("p n t -> p (n t)").bitcast(I32))
+        query2_raw = sb.tile([P, PACK, Q], F32, name="query2_raw", tag="query2_raw", align_bytes=64)
+        nc.sync.dma_start(query2_raw[:], query2.rearrange("(p j) w -> p j w", j=PACK))
         grace_col = sb.tile([P, 1], F32, name="grace_col")
         nc.sync.dma_start(grace_col[:], grace)
+        gout_raw = sb.tile([P, PACK, Q], F32, name="gout_raw", tag="gout_raw", align_bytes=64)
+        nc.sync.dma_start(gout_raw[:], gout.rearrange("(p j) w -> p j w", j=PACK))
+        val_words = sb.tile([P, T], I32, name="val_words", tag="val_words", align_bytes=64)
+        nc.sync.dma_start(val_words[:], vals_words[0].rearrange("p n t -> p (n t)").bitcast(I32))
         gq1_col = sb.tile([P, 1], F32, name="gq1_col")
         nc.sync.dma_start(gq1_col[:], gq1)
         base_sb = sb.tile([P, T], F32, name="base_sb")
         nc.sync.dma_start(base_sb[:], base)
 
-        ones = sb.tile([P, P], F32, name="ones")
-        nc.vector.memset(ones[:], 1.0)
-        warm = sb.tile([P, 1], F32, name="warm")
-        nc.scalar.activation(warm[:], ones[:, 0:1], ACT.Exp)
         quad_start = sb.tile([P, 1], F32, name="quad_start")
         for quad in range(4):
             nc.vector.memset(quad_start[32 * quad : 32 * quad + 32, :], 32.0 * quad)
@@ -82,18 +86,16 @@ def tile_attend_gpsoftlives_b_kernel(tc, query, query2, keys_words, keys_scales,
         nc.vector.scalar_tensor_tensor(ident[:], count[:], quad_start[:], lane[:, 0:1].to_broadcast([P, P]),
                                        ALU.subtract, ALU.is_equal)
 
-        def quantize(raw, name, tag, codes_tag):
-            grouped = sb.tile([P, Q, PACK], BF16, name=name + "_grouped", tag=tag, align_bytes=64)
+        def quantize(raw, name, codes):
+            grouped = sb.tile([P, Q, PACK], BF16, name=name + "_grouped", align_bytes=64)
             nc.scalar.copy(grouped[:].rearrange("p (c i) t -> p c t i", i=4),
                            raw[:].rearrange("p t (c i) -> p c t i", i=4))
-            codes = sb.tile([P, Q], U32, name=name + "_codes", tag=codes_tag, align_bytes=64)
-            scales = sb.tile([P, Q], U8, name=name + "_scales", tag=name + "_scales", align_bytes=64)
+            scales = sb.tile([P, Q], U8, name=name + "_scales", align_bytes=64)
             nc.vector.quantize_mx(out=codes[:].bitcast(FP8X4), scales=scales[:],
                                   in_=grouped[:].rearrange("p w j -> p (w j)"))
             return codes, scales
 
-        def gather(window, dtype, name, tag=None):
-            picked = sb.tile([P, I], dtype, name=name, tag=tag or name, align_bytes=64)
+        def gather(picked, window):
             nc.vector.tensor_copy(picked[:], window.indirect(offsets[:]))
             return picked
 
@@ -109,52 +111,54 @@ def tile_attend_gpsoftlives_b_kernel(tc, query, query2, keys_words, keys_scales,
         def row_tile(name, tag=None):
             return sb.tile([P, I], F32, name=name, tag=tag or name, align_bytes=64)
 
-        key_bytes_g = gather(key_bytes[:], U8, "key_bytes_g")
-        query_mx = quantize(query_raw, "query", "key_words_g", "query_codes")
-
-        size_bank = ps.tile([P, PACK, P], F32, name="size_bank", tag="a_bank")
+        key_bytes_g = gather(sb.tile([P, I], U8, name="key_bytes_g", align_bytes=64), key_bytes[:])
+        query_mx = quantize(query_raw, "query", sb.tile([P, Q], U32, name="query_codes", align_bytes=64))
+        size_bank = ps.tile([P, PACK, P], F32, name="size_bank")
         for j in range(PACK):
             nc.tensor.transpose(size_bank[:, j, :], size_cols[:, j : j + 1].to_broadcast([P, P]), ident[:])
         size_rows = sb.tile([P, P, PACK], F32, name="size_rows")
         nc.scalar.copy(size_rows[:], size_bank[:].rearrange("p j s -> p s j"))
 
-        key_words_g = gather(key_words[:].bitcast(U32), U32, "key_words_g")
-        a_bank = scores(query_mx, key_words_g, key_bytes_g, "a_bank")
-        age_g = gather(age_pool[:], F32, "age_g", "key_words")
-        query2_mx = quantize(query2_raw, "query2", "query2_grouped", "age_pool")
-        b_bank = scores(query2_mx, key_words_g, key_bytes_g, "b_bank")
+        age_g = gather(row_tile("age_g"), age_pool[:])
+        key_words_g = gather(reuse.tile([P, I], U32, name="key_words_g", align_bytes=64, offset=0),
+                             key_words[:].bitcast(U32))
+        val_bytes_g = gather(reuse.tile([P, I], U8, name="val_bytes_g", align_bytes=64, offset=4 * I), val_bytes[:])
 
         age_turn = ps.tile([P, PACK, P], F32, name="age_turn")
         for j in range(PACK):
             nc.tensor.transpose(age_turn[:, j, :], age_g[:, j * P : (j + 1) * P], ident[:])
-        age_cols = sb.tile([P, PACK], F32, name="age_cols", tag="query2_scales", align_bytes=64)
+        age_cols = sb.tile([P, PACK], F32, name="age_cols")
         nc.scalar.copy(age_cols[:], age_turn[:, :, 0])
         age_bank = ps.tile([P, PACK, P], F32, name="age_bank")
         for j in range(PACK):
             nc.tensor.transpose(age_bank[:, j, :], age_cols[:, j : j + 1].to_broadcast([P, P]), ident[:])
 
-        neg_max = column("neg_max", "query2_grouped")
-        neg_a = row_tile("neg_a")
+        a_bank = scores(query_mx, key_words_g, key_bytes_g, "a_bank")
+        neg_max = column("neg_max")
+        neg_a = reuse.tile([P, I], F32, name="neg_a", align_bytes=64, offset=4 * T)
         nc.vector.tensor_scalar(neg_a[:], a_bank[:], -1.0, None, ALU.mult, ALU.min, accum_out=neg_max[:])
-        r = row_tile("r", "gout_raw")
-        b = row_tile("b")
-        val_bytes_g = gather(val_bytes[:], U8, "val_bytes_g", "neg_a")
-        gout_mx = quantize(gout_raw, "gout", "gout_grouped", "val_bytes")
-        nc.scalar.activation(r[:], a_bank[:], ACT.Exp, bias=neg_max[:])
-        nc.scalar.copy(b[:], b_bank[:])
+        query2_mx = quantize(query2_raw, "query2", sb.tile([P, Q], U32, name="query2_codes", align_bytes=64))
+        slack = row_tile("slack", "query2_raw")
+        nc.scalar.activation(slack[:], age_bank[:].rearrange("p j s -> p (j s)"), ACT.Identity,
+                             bias=grace_col[:], scale=-1.0)
+        b_bank = scores(query2_mx, key_words_g, key_bytes_g, "b_bank")
+        gout_mx = quantize(gout_raw, "gout", reuse.tile([P, Q], U32, name="gout_codes", align_bytes=64, offset=4 * T))
 
-        x = row_tile("x", "gout_grouped")
-        nc.vector.scalar_tensor_tensor(x[:], b[:], grace_col[:], age_bank[:].rearrange("p j s -> p (j s)"),
-                                       ALU.add, ALU.subtract)
+        r = row_tile("r", "gout_raw")
+        nc.scalar.activation(r[:], a_bank[:], ACT.Exp, bias=neg_max[:])
+
+        x = row_tile("x")
+        nc.vector.tensor_tensor(x[:], b_bank[:], slack[:], ALU.add)
         life = row_tile("life")
         nc.scalar.activation(life[:], x[:], ACT.Sigmoid, scale=3.0)
         death = row_tile("death")
         nc.scalar.activation(death[:], x[:], ACT.Sigmoid, scale=-3.0)
 
-        val_words_g = gather(val_words[:].bitcast(U32), U32, "val_words_g", "b")
+        val_words_g = gather(reuse.tile([P, I], U32, name="val_words_g", align_bytes=64, offset=4 * T + 4 * Q),
+                             val_words[:].bitcast(U32))
         c_bank = scores(gout_mx, val_words_g, val_bytes_g, "c_bank")
 
-        placed = sb.tile([P, T], F32, name="placed", tag="b", align_bytes=64)
+        placed = reuse.tile([P, T], F32, name="placed", align_bytes=64, offset=4 * T + 4 * Q)
         nc.gpsimd.memset(placed[:], 0.0)
 
         neg_gain = column("neg_gain")
@@ -168,16 +172,21 @@ def tile_attend_gpsoftlives_b_kernel(tc, query, query2, keys_words, keys_scales,
         bend = row_tile("bend")
         nc.scalar.activation(bend[:], life[:], ACT.Identity, bias=-1.0, scale=2.0)
 
-        c = row_tile("c", "gout_raw")
-        nc.vector.tensor_tensor(c[:], c_bank[:], size_rows[:].rearrange("p s j -> p (s j)"), ALU.mult)
+        halves = [slice(0, I // 2), slice(I // 2, I)]
+        size_flat = size_rows[:].rearrange("p s j -> p (s j)")
+        c = row_tile("c", "x")
+        for half in halves:
+            nc.vector.tensor_tensor(c[:, half], c_bank[:, half], size_flat[:, half], ALU.mult)
 
         u = row_tile("u")
-        nc.vector.scalar_tensor_tensor(u[:], p[:], inv_z[:], death[:], ALU.mult, ALU.mult)
         mean = column("mean")
         cp = row_tile("cp")
         nc.vector.scalar_tensor_tensor(cp[:], p[:], inv_z[:], c[:], ALU.mult, ALU.mult, accum_out=mean[:])
+        for half in halves:
+            nc.vector.scalar_tensor_tensor(u[:, half], p[:, half], inv_z[:], death[:, half], ALU.mult, ALU.mult)
         v = row_tile("v")
-        nc.vector.scalar_tensor_tensor(v[:], c[:], mean[:], u[:], ALU.subtract, ALU.mult)
+        for half in halves:
+            nc.vector.scalar_tensor_tensor(v[:, half], c[:, half], mean[:], u[:, half], ALU.subtract, ALU.mult)
         gain_u = row_tile("gain_u")
         nc.scalar.activation(gain_u[:], u[:], ACT.Copy, scale=neg_gain[:])
 
@@ -191,9 +200,11 @@ def tile_attend_gpsoftlives_b_kernel(tc, query, query2, keys_words, keys_scales,
         vu = row_tile("vu")
         nc.vector.scalar_tensor_tensor(vu[:], v[:], neg_gain[:], u[:], ALU.mult, ALU.mult, accum_out=sum_vu[:])
         k = row_tile("k")
-        nc.vector.scalar_tensor_tensor(k[:], v[:], neg_gain[:], bend[:], ALU.mult, ALU.mult)
+        for half in halves:
+            nc.vector.scalar_tensor_tensor(k[:, half], v[:, half], neg_gain[:], bend[:, half], ALU.mult, ALU.mult)
         head = row_tile("head")
-        nc.vector.scalar_tensor_tensor(head[:], k[:], sum_vu[:], v[:], ALU.add, ALU.mult)
+        for half in halves:
+            nc.vector.scalar_tensor_tensor(head[:, half], k[:, half], sum_vu[:], v[:, half], ALU.add, ALU.mult)
         nc.vector.tensor_tensor(placed[:].indirect(offsets[:]), head[:], tail[:], ALU.add)
 
         start = 0

@@ -36,10 +36,10 @@ def tile_attend_gpsoftlives_b_kernel(tc, query, query2, keys_words, keys_scales,
         size_cols = sb.tile([P, PACK], F32, name="size_cols")
         nc.sync.dma_start(size_cols[:], size.rearrange("o (p j) -> (o p) j", j=PACK))
 
-        ones = sb.tile([P, P], F32, name="ones")
+        ones = sb.tile([P, P + 1], F32, name="ones")
         nc.vector.memset(ones[:], 1.0)
         warm = sb.tile([P, 1], F32, name="warm")
-        nc.scalar.activation(warm[:], ones[:, 0:1], ACT.Exp)
+        nc.scalar.activation(warm[:], ones[:, P : P + 1], ACT.Exp)
 
         key_bytes = sb.tile([P, T], U8, name="key_bytes", align_bytes=64)
         val_bytes = sb.tile([P, T], U8, name="val_bytes", tag="val_bytes", align_bytes=64)
@@ -61,15 +61,15 @@ def tile_attend_gpsoftlives_b_kernel(tc, query, query2, keys_words, keys_scales,
         nc.sync.dma_start(age_pool[0:1, :], age[0:1, :])
         key_words = sb.tile([P, T], I32, name="key_words", align_bytes=64)
         nc.sync.dma_start(key_words[:], keys_words[0].rearrange("p n t -> p (n t)").bitcast(I32))
-        load_scale_rows(val_bytes, vals_scales)
-        query2_raw = sb.tile([P, PACK, Q], F32, name="query2_raw", tag="query2_raw", align_bytes=64)
+        query2_raw = reuse.tile([P, PACK, Q], F32, name="query2_raw", align_bytes=64, offset=4 * T + 4 * I)
         nc.sync.dma_start(query2_raw[:], query2.rearrange("(p j) w -> p j w", j=PACK))
-        grace_col = sb.tile([P, 1], F32, name="grace_col")
-        nc.sync.dma_start(grace_col[:], grace)
+        load_scale_rows(val_bytes, vals_scales)
         gout_raw = sb.tile([P, PACK, Q], F32, name="gout_raw", tag="gout_raw", align_bytes=64)
         nc.sync.dma_start(gout_raw[:], gout.rearrange("(p j) w -> p j w", j=PACK))
         val_words = sb.tile([P, T], I32, name="val_words", tag="val_words", align_bytes=64)
         nc.sync.dma_start(val_words[:], vals_words[0].rearrange("p n t -> p (n t)").bitcast(I32))
+        grace_col = sb.tile([P, 1], F32, name="grace_col")
+        nc.sync.dma_start(grace_col[:], grace)
         gq1_col = sb.tile([P, 1], F32, name="gq1_col")
         nc.sync.dma_start(gq1_col[:], gq1)
         base_sb = sb.tile([P, T], F32, name="base_sb")
@@ -79,7 +79,7 @@ def tile_attend_gpsoftlives_b_kernel(tc, query, query2, keys_words, keys_scales,
         for quad in range(4):
             nc.vector.memset(quad_start[32 * quad : 32 * quad + 32, :], 32.0 * quad)
         count = sb.tile([P, P], F32, name="count", align_bytes=64)
-        nc.vector.tensor_tensor_scan(count[:], ones[:], ones[:], 0.0, ALU.mult, ALU.add)
+        nc.vector.tensor_tensor_scan(count[:], ones[:, :P], ones[:, :P], 0.0, ALU.mult, ALU.add)
         lane = sb.tile([P, 32], F32, name="lane", align_bytes=64)
         nc.vector.transpose(lane[:], count[:, 0:32])
         ident = sb.tile([P, P], F32, name="ident")
@@ -88,8 +88,7 @@ def tile_attend_gpsoftlives_b_kernel(tc, query, query2, keys_words, keys_scales,
 
         def quantize(raw, name, codes):
             grouped = sb.tile([P, Q, PACK], BF16, name=name + "_grouped", align_bytes=64)
-            nc.scalar.copy(grouped[:].rearrange("p (c i) t -> p c t i", i=4),
-                           raw[:].rearrange("p t (c i) -> p c t i", i=4))
+            nc.scalar.copy(grouped[:], raw[:].rearrange("p t c -> p c t"))
             scales = sb.tile([P, Q], U8, name=name + "_scales", align_bytes=64)
             nc.vector.quantize_mx(out=codes[:].bitcast(FP8X4), scales=scales[:],
                                   in_=grouped[:].rearrange("p w j -> p (w j)"))
@@ -112,7 +111,6 @@ def tile_attend_gpsoftlives_b_kernel(tc, query, query2, keys_words, keys_scales,
             return sb.tile([P, I], F32, name=name, tag=tag or name, align_bytes=64)
 
         key_bytes_g = gather(sb.tile([P, I], U8, name="key_bytes_g", align_bytes=64), key_bytes[:])
-        query_mx = quantize(query_raw, "query", sb.tile([P, Q], U32, name="query_codes", align_bytes=64))
         size_bank = ps.tile([P, PACK, P], F32, name="size_bank")
         for j in range(PACK):
             nc.tensor.transpose(size_bank[:, j, :], size_cols[:, j : j + 1].to_broadcast([P, P]), ident[:])
@@ -120,11 +118,12 @@ def tile_attend_gpsoftlives_b_kernel(tc, query, query2, keys_words, keys_scales,
         nc.scalar.copy(size_rows[:], size_bank[:].rearrange("p j s -> p s j"))
 
         age_g = gather(row_tile("age_g"), age_pool[:])
+        query_mx = quantize(query_raw, "query", reuse.tile([P, Q], U32, name="query_codes", align_bytes=64, offset=5 * I))
         key_words_g = gather(reuse.tile([P, I], U32, name="key_words_g", align_bytes=64, offset=0),
                              key_words[:].bitcast(U32))
         val_bytes_g = gather(reuse.tile([P, I], U8, name="val_bytes_g", align_bytes=64, offset=4 * I), val_bytes[:])
 
-        age_turn = ps.tile([P, PACK, P], F32, name="age_turn")
+        age_turn = ps.tile([P, PACK, P], F32, name="age_turn", tag="a_bank")
         for j in range(PACK):
             nc.tensor.transpose(age_turn[:, j, :], age_g[:, j * P : (j + 1) * P], ident[:])
         age_cols = sb.tile([P, PACK], F32, name="age_cols")
@@ -134,37 +133,42 @@ def tile_attend_gpsoftlives_b_kernel(tc, query, query2, keys_words, keys_scales,
             nc.tensor.transpose(age_bank[:, j, :], age_cols[:, j : j + 1].to_broadcast([P, P]), ident[:])
 
         a_bank = scores(query_mx, key_words_g, key_bytes_g, "a_bank")
+        query2_mx = quantize(query2_raw, "query2", sb.tile([P, Q], U32, name="query2_codes", align_bytes=64))
+        b_bank = scores(query2_mx, key_words_g, key_bytes_g, "b_bank")
+        age_rows = reuse.tile([P, I], F32, name="age_rows", align_bytes=64, offset=4 * T + 4 * I)
+        nc.scalar.copy(age_rows[:], age_bank[:].rearrange("p j s -> p (j s)"))
+
         neg_max = column("neg_max")
         neg_a = reuse.tile([P, I], F32, name="neg_a", align_bytes=64, offset=4 * T)
         nc.vector.tensor_scalar(neg_a[:], a_bank[:], -1.0, None, ALU.mult, ALU.min, accum_out=neg_max[:])
-        query2_mx = quantize(query2_raw, "query2", sb.tile([P, Q], U32, name="query2_codes", align_bytes=64))
-        slack = row_tile("slack", "query2_raw")
-        nc.scalar.activation(slack[:], age_bank[:].rearrange("p j s -> p (j s)"), ACT.Identity,
-                             bias=grace_col[:], scale=-1.0)
-        b_bank = scores(query2_mx, key_words_g, key_bytes_g, "b_bank")
         gout_mx = quantize(gout_raw, "gout", reuse.tile([P, Q], U32, name="gout_codes", align_bytes=64, offset=4 * T))
-
         r = row_tile("r", "gout_raw")
         nc.scalar.activation(r[:], a_bank[:], ACT.Exp, bias=neg_max[:])
 
         x = row_tile("x")
-        nc.vector.tensor_tensor(x[:], b_bank[:], slack[:], ALU.add)
+        nc.vector.scalar_tensor_tensor(x[:], b_bank[:], grace_col[:], age_rows[:], ALU.add, ALU.subtract)
+
+        halves = [slice(0, I // 2), slice(I // 2, I)]
+        c_bank = ps.tile([P, I], F32, name="c_bank")
+        for n, half in enumerate(halves):
+            words = reuse.tile([P, I // 2], U32, name="val_words_g%d" % n, align_bytes=64,
+                               offset=4 * T + [4 * Q, 4 * I][n])
+            nc.vector.tensor_copy(words[:], val_words[:].bitcast(U32).indirect(offsets[:, 16 * n : 16 * n + 16]))
+            nc.tensor.matmul_mx(out=c_bank[:, half], lhsT=gout_mx[0][:].bitcast(FP8X4), lhsT_scale=gout_mx[1][:],
+                                rhs=words[:].bitcast(FP8X4), rhs_scale=val_bytes_g[:, half], start=True, stop=True)
+
         life = row_tile("life")
         nc.scalar.activation(life[:], x[:], ACT.Sigmoid, scale=3.0)
         death = row_tile("death")
         nc.scalar.activation(death[:], x[:], ACT.Sigmoid, scale=-3.0)
 
-        val_words_g = gather(reuse.tile([P, I], U32, name="val_words_g", align_bytes=64, offset=4 * T + 4 * Q),
-                             val_words[:].bitcast(U32))
-        c_bank = scores(gout_mx, val_words_g, val_bytes_g, "c_bank")
-
-        placed = reuse.tile([P, T], F32, name="placed", align_bytes=64, offset=4 * T + 4 * Q)
+        placed = reuse.tile([P, T], F32, name="placed", align_bytes=64, offset=4 * T + 4 * I)
         nc.gpsimd.memset(placed[:], 0.0)
 
         neg_gain = column("neg_gain")
         nc.scalar.activation(neg_gain[:], gq1_col[:], ACT.Copy, scale=-PENALTY)
 
-        p = row_tile("p", "val_words")
+        p = row_tile("p")
         z = column("z")
         nc.vector.scalar_tensor_tensor(p[:], r[:], 1.0, life[:], ALU.mult, ALU.mult, accum_out=z[:])
         inv_z = column("inv_z")
@@ -172,7 +176,6 @@ def tile_attend_gpsoftlives_b_kernel(tc, query, query2, keys_words, keys_scales,
         bend = row_tile("bend")
         nc.scalar.activation(bend[:], life[:], ACT.Identity, bias=-1.0, scale=2.0)
 
-        halves = [slice(0, I // 2), slice(I // 2, I)]
         size_flat = size_rows[:].rearrange("p s j -> p (s j)")
         c = row_tile("c", "x")
         for half in halves:

from contextlib import ExitStack

import concourse.mybir as mybir

D, E, T, I, Q = 512, 512, 2048, 512, 128
FLOPS = 3 * 2 * 512 * 512 * 128

F32 = mybir.dt.float32
BF16 = mybir.dt.bfloat16
I32 = mybir.dt.int32
U32 = mybir.dt.uint32
U16 = mybir.dt.uint16
U8 = mybir.dt.uint8
FP8X4 = mybir.dt.float8_e4m3fn_x4
ALU = mybir.AluOpType
ACT = mybir.ActivationFunctionType

P = 128
PACK = 4
PENALTY = 27.0 * 2.0 * 512.0 * 512.0
AGE_SPLIT = 1024
STORE_WIDTHS = [256, 512, 512, 512, 256]


def tile_attend_gpsoftlives_b_kernel(tc, query, query2, keys_words, keys_scales, age, grace, gout,
                                      vals_words, vals_scales, size, base, gq1, offs, out):
    nc = tc.nc
    with ExitStack() as ctx:
        sb = ctx.enter_context(tc.tile_pool(name="sb", bufs=1))
        reuse = ctx.enter_context(tc.tile_pool(name="reuse", bufs=1))
        ps = ctx.enter_context(tc.psum_pool(name="ps", bufs=1))

        offsets = sb.tile([P, I // 16], U16, name="offsets")
        nc.sync.dma_start(offsets[:], offs)

        size_cols = sb.tile([P, PACK], F32, name="size_cols")
        nc.sync.dma_start(size_cols[:], size.rearrange("o (p j) -> (o p) j", j=PACK))

        ones = sb.tile([P, P + 1], F32, name="ones")
        nc.vector.memset(ones[:], 1.0)
        warm = sb.tile([P, 1], F32, name="warm")
        nc.scalar.activation(warm[:], ones[:, P : P + 1], ACT.Exp)

        key_bytes = sb.tile([P, T], U8, name="key_bytes", align_bytes=64)
        val_bytes = sb.tile([P, T], U8, name="val_bytes", tag="val_bytes", align_bytes=64)
        age_pool = reuse.tile([P, T], F32, name="age_pool", align_bytes=64, offset=0)
        nc.gpsimd.memset(key_bytes[:].bitcast(I32), 0)
        nc.vector.memset(age_pool[:, : AGE_SPLIT - 1], 0.0)
        nc.vector.memset(age_pool[:, AGE_SPLIT - 1 : AGE_SPLIT], 0.0)
        nc.gpsimd.memset(age_pool[:, AGE_SPLIT:], 0.0)
        nc.gpsimd.memset(val_bytes[:].bitcast(I32), 0)

        def load_scale_rows(tile, scales):
            for quad in range(4):
                nc.sync.dma_start(tile[32 * quad : 32 * quad + 4, :].bitcast(I32),
                                  scales[0, 4 * quad : 4 * quad + 4, :].bitcast(I32))

        load_scale_rows(key_bytes, keys_scales)
        query_raw = sb.tile([P, PACK, Q], F32, name="query_raw")
        nc.sync.dma_start(query_raw[:], query.rearrange("(p j) w -> p j w", j=PACK))
        nc.sync.dma_start(age_pool[0:1, :], age[0:1, :])
        key_words = sb.tile([P, T], I32, name="key_words", align_bytes=64)
        nc.sync.dma_start(key_words[:], keys_words[0].rearrange("p n t -> p (n t)").bitcast(I32))
        query2_raw = reuse.tile([P, PACK, Q], F32, name="query2_raw", align_bytes=64, offset=4 * T + 4 * I)
        nc.sync.dma_start(query2_raw[:], query2.rearrange("(p j) w -> p j w", j=PACK))
        load_scale_rows(val_bytes, vals_scales)
        gout_raw = sb.tile([P, PACK, Q], F32, name="gout_raw", tag="gout_raw", align_bytes=64)
        nc.sync.dma_start(gout_raw[:], gout.rearrange("(p j) w -> p j w", j=PACK))
        val_words = sb.tile([P, T], I32, name="val_words", tag="val_words", align_bytes=64)
        nc.sync.dma_start(val_words[:], vals_words[0].rearrange("p n t -> p (n t)").bitcast(I32))
        grace_col = sb.tile([P, 1], F32, name="grace_col")
        nc.sync.dma_start(grace_col[:], grace)
        gq1_col = sb.tile([P, 1], F32, name="gq1_col")
        nc.sync.dma_start(gq1_col[:], gq1)
        base_sb = sb.tile([P, T], F32, name="base_sb")
        nc.sync.dma_start(base_sb[:], base)

        quad_start = sb.tile([P, 1], F32, name="quad_start")
        for quad in range(4):
            nc.vector.memset(quad_start[32 * quad : 32 * quad + 32, :], 32.0 * quad)
        count = sb.tile([P, P], F32, name="count", align_bytes=64)
        nc.vector.tensor_tensor_scan(count[:], ones[:, :P], ones[:, :P], 0.0, ALU.mult, ALU.add)
        lane = sb.tile([P, 32], F32, name="lane", align_bytes=64)
        nc.vector.transpose(lane[:], count[:, 0:32])
        ident = sb.tile([P, P], F32, name="ident")
        nc.vector.scalar_tensor_tensor(ident[:], count[:], quad_start[:], lane[:, 0:1].to_broadcast([P, P]),
                                       ALU.subtract, ALU.is_equal)

        def quantize(raw, name, codes):
            grouped = sb.tile([P, Q, PACK], BF16, name=name + "_grouped", align_bytes=64)
            nc.scalar.copy(grouped[:], raw[:].rearrange("p t c -> p c t"))
            scales = sb.tile([P, Q], U8, name=name + "_scales", align_bytes=64)
            nc.vector.quantize_mx(out=codes[:].bitcast(FP8X4), scales=scales[:],
                                  in_=grouped[:].rearrange("p w j -> p (w j)"))
            return codes, scales

        def gather(picked, window):
            nc.vector.tensor_copy(picked[:], window.indirect(offsets[:]))
            return picked

        def scores(rows, words, scale_bytes, name):
            bank = ps.tile([P, I], F32, name=name, tag=name)
            nc.tensor.matmul_mx(out=bank[:], lhsT=rows[0][:].bitcast(FP8X4), lhsT_scale=rows[1][:],
                                rhs=words[:].bitcast(FP8X4), rhs_scale=scale_bytes[:], start=True, stop=True)
            return bank

        def column(name, tag=None):
            return sb.tile([P, 1], F32, name=name, tag=tag or name, align_bytes=64)

        def row_tile(name, tag=None):
            return sb.tile([P, I], F32, name=name, tag=tag or name, align_bytes=64)

        key_bytes_g = gather(sb.tile([P, I], U8, name="key_bytes_g", align_bytes=64), key_bytes[:])
        size_bank = ps.tile([P, PACK, P], F32, name="size_bank")
        for j in range(PACK):
            nc.tensor.transpose(size_bank[:, j, :], size_cols[:, j : j + 1].to_broadcast([P, P]), ident[:])
        size_rows = sb.tile([P, P, PACK], F32, name="size_rows")
        nc.scalar.copy(size_rows[:], size_bank[:].rearrange("p j s -> p s j"))

        age_g = gather(row_tile("age_g"), age_pool[:])
        query_mx = quantize(query_raw, "query", reuse.tile([P, Q], U32, name="query_codes", align_bytes=64, offset=5 * I))
        key_words_g = gather(reuse.tile([P, I], U32, name="key_words_g", align_bytes=64, offset=0),
                             key_words[:].bitcast(U32))
        val_bytes_g = gather(reuse.tile([P, I], U8, name="val_bytes_g", align_bytes=64, offset=4 * I), val_bytes[:])

        age_turn = ps.tile([P, PACK, P], F32, name="age_turn", tag="a_bank")
        for j in range(PACK):
            nc.tensor.transpose(age_turn[:, j, :], age_g[:, j * P : (j + 1) * P], ident[:])
        age_cols = sb.tile([P, PACK], F32, name="age_cols")
        nc.scalar.copy(age_cols[:], age_turn[:, :, 0])
        age_bank = ps.tile([P, PACK, P], F32, name="age_bank")
        for j in range(PACK):
            nc.tensor.transpose(age_bank[:, j, :], age_cols[:, j : j + 1].to_broadcast([P, P]), ident[:])

        a_bank = scores(query_mx, key_words_g, key_bytes_g, "a_bank")
        query2_mx = quantize(query2_raw, "query2", sb.tile([P, Q], U32, name="query2_codes", align_bytes=64))
        b_bank = scores(query2_mx, key_words_g, key_bytes_g, "b_bank")
        age_rows = reuse.tile([P, I], F32, name="age_rows", align_bytes=64, offset=4 * T + 4 * I)
        nc.scalar.copy(age_rows[:], age_bank[:].rearrange("p j s -> p (j s)"))

        neg_max = column("neg_max")
        neg_a = reuse.tile([P, I], F32, name="neg_a", align_bytes=64, offset=4 * T)
        nc.vector.tensor_scalar(neg_a[:], a_bank[:], -1.0, None, ALU.mult, ALU.min, accum_out=neg_max[:])
        gout_mx = quantize(gout_raw, "gout", reuse.tile([P, Q], U32, name="gout_codes", align_bytes=64, offset=4 * T))
        r = row_tile("r", "gout_raw")
        nc.scalar.activation(r[:], a_bank[:], ACT.Exp, bias=neg_max[:])

        x = row_tile("x")
        nc.vector.scalar_tensor_tensor(x[:], b_bank[:], grace_col[:], age_rows[:], ALU.add, ALU.subtract)

        halves = [slice(0, I // 2), slice(I // 2, I)]
        c_bank = ps.tile([P, I], F32, name="c_bank")
        for n, half in enumerate(halves):
            words = reuse.tile([P, I // 2], U32, name="val_words_g%d" % n, align_bytes=64,
                               offset=4 * T + [4 * Q, 4 * I][n])
            nc.vector.tensor_copy(words[:], val_words[:].bitcast(U32).indirect(offsets[:, 16 * n : 16 * n + 16]))
            nc.tensor.matmul_mx(out=c_bank[:, half], lhsT=gout_mx[0][:].bitcast(FP8X4), lhsT_scale=gout_mx[1][:],
                                rhs=words[:].bitcast(FP8X4), rhs_scale=val_bytes_g[:, half], start=True, stop=True)

        life = row_tile("life")
        nc.scalar.activation(life[:], x[:], ACT.Sigmoid, scale=3.0)
        death = row_tile("death")
        nc.scalar.activation(death[:], x[:], ACT.Sigmoid, scale=-3.0)

        placed = reuse.tile([P, T], F32, name="placed", align_bytes=64, offset=4 * T + 4 * I)
        nc.gpsimd.memset(placed[:], 0.0)

        neg_gain = column("neg_gain")
        nc.scalar.activation(neg_gain[:], gq1_col[:], ACT.Copy, scale=-PENALTY)

        p = row_tile("p")
        z = column("z")
        nc.vector.scalar_tensor_tensor(p[:], r[:], 1.0, life[:], ALU.mult, ALU.mult, accum_out=z[:])
        inv_z = column("inv_z")
        nc.vector.reciprocal(inv_z[:], z[:])
        bend = row_tile("bend")
        nc.scalar.activation(bend[:], life[:], ACT.Identity, bias=-1.0, scale=2.0)

        size_flat = size_rows[:].rearrange("p s j -> p (s j)")
        c = row_tile("c", "x")
        for half in halves:
            nc.vector.tensor_tensor(c[:, half], c_bank[:, half], size_flat[:, half], ALU.mult)

        u = row_tile("u")
        mean = column("mean")
        cp = row_tile("cp")
        nc.vector.scalar_tensor_tensor(cp[:], p[:], inv_z[:], c[:], ALU.mult, ALU.mult, accum_out=mean[:])
        for half in halves:
            nc.vector.scalar_tensor_tensor(u[:, half], p[:, half], inv_z[:], death[:, half], ALU.mult, ALU.mult)
        v = row_tile("v")
        for half in halves:
            nc.vector.scalar_tensor_tensor(v[:, half], c[:, half], mean[:], u[:, half], ALU.subtract, ALU.mult)
        gain_u = row_tile("gain_u")
        nc.scalar.activation(gain_u[:], u[:], ACT.Copy, scale=neg_gain[:])

        sum_vv = column("sum_vv")
        vv = row_tile("vv")
        nc.scalar.activation(vv[:], v[:], ACT.Square, accum_out=sum_vv[:])
        tail = row_tile("tail")
        nc.scalar.activation(tail[:], gain_u[:], ACT.Copy, scale=sum_vv[:])

        sum_vu = column("sum_vu")
        vu = row_tile("vu")
        nc.vector.scalar_tensor_tensor(vu[:], v[:], neg_gain[:], u[:], ALU.mult, ALU.mult, accum_out=sum_vu[:])
        k = row_tile("k")
        for half in halves:
            nc.vector.scalar_tensor_tensor(k[:, half], v[:, half], neg_gain[:], bend[:, half], ALU.mult, ALU.mult)
        head = row_tile("head")
        for half in halves:
            nc.vector.scalar_tensor_tensor(head[:, half], k[:, half], sum_vu[:], v[:, half], ALU.add, ALU.mult)
        nc.vector.tensor_tensor(placed[:].indirect(offsets[:]), head[:], tail[:], ALU.add)

        start = 0
        for n, width in enumerate(STORE_WIDTHS):
            cols = slice(start, start + width)
            total = sb.tile([P, width], F32, name="total%d" % n)
            nc.vector.tensor_tensor(total[:], placed[:, cols], base_sb[:, cols], ALU.add)
            nc.sync.dma_start(out[:, cols], total[:])
            start = start + width
